import numpy as np
CORES = [65,73,81,89,97,105,113,121]
N = 8
R, W, T = 16384, 64, 512
CAPP = 128
def entries(a): return a.T.reshape(-1)
def pack(v, P): return np.ascontiguousarray(np.asarray(v, np.int32).reshape(-1, P).T)
def lists(rng, how):
    I = rng.integers(0, N * R, (N, T))
    O = np.stack([rng.permutation(np.repeat(np.arange(N), CAPP))[:T] for r in range(N)])
    if how == "full": O = np.stack([rng.permutation(np.repeat(rng.permutation(N)[:T // CAPP], CAPP)) for r in range(N)])
    I = R * O + rng.integers(0, R, (N, T))
    if how == "alike": I = R * O + rng.integers(0, R)
    if how == "edge": I = R * O + np.where(rng.random((N, T)) < 0.5, 0, R - 1)
    if how == "sorted": I = np.sort(I, axis=1)
    return {"idx": np.stack([pack(I[r], 128) for r in range(N)])}
def setup_inputs(rng):
    return dict({"gr": rng.standard_normal((N, T, W), dtype=np.float32)}, **lists(rng, "uniform"))
def setup_inputs_alike(rng):
    d = setup_inputs(rng); d.update(lists(rng, "alike"))
    for k in ("gr",): d[k] = (d[k].astype(np.float32) * 1024.0).astype(d[k].dtype)
    return d
def setup_inputs_edge(rng):
    d = setup_inputs(rng); d.update(lists(rng, "edge"))
    for k in ("gr",): d[k] = (d[k].astype(np.float32) * (1 / 1024.0)).astype(d[k].dtype)
    return d
def setup_inputs_full(rng):
    d = setup_inputs(rng); d.update(lists(rng, "full"))
    return d
def setup_inputs_sorted(rng):
    d = setup_inputs(rng); d.update(lists(rng, "sorted"))
    return d
def check_inputs(x):
    bad = []
    if x["idx"].min() < 0 or x["idx"].max() >= N * R: bad.append("idx out of range")
    if max(int(np.bincount(entries(a) // R, minlength=N).max()) for a in x["idx"]) > CAPP: bad.append("more than CAPP entries of a list point into one rank's part")
    return bad
def reference(gr, idx):
    A = np.zeros((N * R, W))
    for r in range(N):
        np.add.at(A, entries(idx[r]), gr[r].astype(np.float64))
    return {"y": np.stack([A[R * r:R * r + R] for r in range(N)]).astype(np.float32)}

@@ -1,0 +1,338 @@
+from concourse.bass import IndirectOffsetOnAxis
+from concourse.mybir import AluOpType, ActivationFunctionType
+
+P128 = 128
+CW = 68
+NB = 65
+NSL = 16
+FLY = 3
+
+SCRATCH = {
+    "idxs": ("sbuf", [128, 4], "int32"),
+    "owni": ("sbuf", [128, 4], "int32"),
+    "loci": ("sbuf", [128, 4], "int32"),
+    "ownf": ("sbuf", [128, 4], "float32"),
+    "raw": ("sbuf", [128, 4 * CW], "float32"),
+    "io8": ("sbuf", [128, 8], "float32"),
+    "io1": ("sbuf", [128, 128], "float32"),
+    "onesf": ("sbuf", [128, 128], "float32"),
+    "onesb": ("sbuf", [128, 128], "bfloat16"),
+    "lb": ("sbuf", [128, 128], "bfloat16"),
+    "ident": ("sbuf", [128, 128], "float32"),
+    "mle": ("sbuf", [128, 128], "float32"),
+    "oh8": ("sbuf", [128, 32], "bfloat16"),
+    "place": ("sbuf", [128, 32], "float32"),
+    "pmat": ("sbuf", [128, 32 * 128], "float32"),
+    "sendb": ("sbuf", [128, 8 * CW], "float32"),
+    "land": ("sbuf", [128, 8 * CW], "float32"),
+    "fw": ("sbuf", [128, NB], "float32"),
+    "diag": ("sbuf", [128, 1024], "float32"),
+    "rowb": ("sbuf", [128, 1024], "float32"),
+    "eq": ("sbuf", [128, 36 * 128], "float32"),
+    "junk": ("sbuf", [128, 36 * 128], "float32"),
+    "cnt": ("sbuf", [128, 8], "float32"),
+    "fl": ("sbuf", [128, 8], "float32"),
+    "sel": ("sbuf", [128, 8], "float32"),
+    "sidx": ("sbuf", [128, 8], "int32"),
+    "outb": ("sbuf", [128, 512], "float32"),
+    "z": ("sbuf", [128, 2048], "float32"),
+    "ppre": ("psum", [128, 512], "float32"),
+    "pc0": ("psum", [128, 512], "float32"),
+    "pc1": ("psum", [128, 512], "float32"),
+    "pb0": ("psum", [128, 512], "float32"),
+    "pb1": ("psum", [128, 512], "float32"),
+    "pg0": ("psum", [128, 512], "float32"),
+    "pg1": ("psum", [128, 512], "float32"),
+    "pg2": ("psum", [128, 512], "float32"),
+}
+SEMAPHORES = ["sv", "sp", "ss", "sg", "lidx", "lgr", "zs0", "zs1", "zs2", "sent", "fin", "fout", "sc"] + \
+             ["arr%d" % s for s in range(8)]
+
+
+def _low(mask, n):
+    out, k, b = 0, 0, 0
+    while k < n:
+        if (mask >> b) & 1:
+            out |= 1 << b
+            k += 1
+        b += 1
+    return out
+
+
+def rank_program(g, core, T, topo):
+    cores = [int(c) for c in T.cores]
+    N = len(cores)
+    S = T.sem
+    NE = 8
+    A = AluOpType
+    ACT = ActivationFunctionType
+
+    def split(r):
+        me = cores[r]
+        far = sorted([d for d in range(N) if d != r and not topo.may_write(me, cores[d])], key=lambda d: (d - r) % N)
+        near = sorted([d for d in range(N) if d != r and topo.may_write(me, cores[d])], key=lambda d: (d - r) % N)
+        return far, near
+
+    def send_order(r):
+        far, near = split(r)
+        return far + near + [r]
+
+    def forwarder(r, d):
+        me = cores[r]
+        far, _ = split(r)
+        hs = [h for h in range(topo.CORES_PER_CHIP * topo.CHIPS)
+              if topo.chip(h) == topo.chip(me) and T.rank_of(h) is None and topo.may_write(h, cores[d])]
+        return hs[far.index(d) % len(hs)]
+
+    def chunks(x):
+        est = {}
+        for s in range(N):
+            hop = 0.0 if s == x else (3.0 if topo.may_write(cores[s], cores[x]) else 5.5)
+            est[s] = send_order(s).index(x) * 0.9 + hop
+        return sorted(range(N), key=lambda s: (est[s], s))
+
+    def write(dst, out_ap, in_ap, rsem, lsem):
+        rid, pid, _ = topo.addr(dst)
+        g.remote_dma(out_ap=out_ap, in_ap=in_ap, remote_sem=rsem, local_sem=lsem, pid=pid, routing_id=rid,
+                     dma_engine_mask=_low(topo.mask(core, dst), NE))
+
+    rank = T.rank_of(core)
+    if rank is None:
+        for r in range(N):
+            if topo.chip(cores[r]) != topo.chip(core):
+                continue
+            for d in split(r)[0]:
+                if forwarder(r, d) == core:
+                    k = chunks(d).index(r)
+                    g.wait_ge(S.fin, NE)
+                    write(cores[d], T.land[:, k * CW:k * CW + NB], T.fw[:], S["arr%d" % r], S.fout)
+                    g.wait_ge(S.fout, NE)
+        return
+
+    Q = {"v": g.vector, "p": g.tensor, "s": g.scalar, "g": g, "y": g.sync}
+    SQ = {"v": S.sv, "p": S.sp, "s": S.ss, "g": S.sg}
+    num = {"v": 0, "p": 0, "s": 0, "g": 0}
+    seen = {}
+
+    def done(q, ins):
+        num[q] += 1
+        ins.then_inc(SQ[q], 1)
+        return (q, num[q])
+
+    def need(q, *tickets):
+        for (src, val) in tickets:
+            if seen.get((q, src), 0) < val:
+                Q[q].wait_ge(SQ[src], val)
+                seen[(q, src)] = val
+
+    def need_sem(q, name, val):
+        if seen.get((q, name), 0) < val:
+            Q[q].wait_ge(S[name], val)
+            seen[(q, name)] = val
+
+    V, PE, SC = g.vector, g.tensor, g.scalar
+
+    g.sync.dma_start(T.idxs[:], T.idx[:]).then_inc(S.lidx, 16)
+    for c in range(4):
+        SC.dma_start(T.raw[:, c * CW:c * CW + 64], T.gr[c * 128:(c + 1) * 128, :]).then_inc(S.lgr, 16)
+    t_z = done("v", V.memset(T.z[:, 0:512], 0.0))
+    t_ob = done("v", V.memset(T.onesb[:], 1.0))
+    t_of = done("v", V.memset(T.onesf[:], 1.0))
+    need("s", t_z)
+    for k in range(1, 4):
+        t_ze = done("s", SC.activation(T.z[0:32, 512 * k:512 * (k + 1)], T.z[0:32, 0:512], ACT.Copy))
+    t_io8 = done("g", g.iota(T.io8[:], [[1, 8]], 0, 0, allow_small_or_imprecise_dtypes=True))
+    need("g", t_ob)
+    t_lb = done("g", g.affine_select(T.lb[:], T.onesb[:], [[1, 128]], A.is_ge, 0.0, 0, -1))
+    t_io1 = done("g", g.iota(T.io1[:], [[1, 128]], 1, 0, allow_small_or_imprecise_dtypes=True))
+    need("g", t_of)
+    t_id = done("g", g.affine_select(T.ident[:], T.onesf[:], [[-1, 128]], A.is_equal, 0.0, 0, 1))
+    t_mle = done("g", g.affine_select(T.mle[:], T.onesf[:], [[-1, 128]], A.is_ge, 0.0, 0, 1))
+
+    rows = T.y.shape[0] // NSL
+    ztot = [0] * FLY
+    need("y", t_z)
+    for i in range(NSL):
+        j = i % FLY
+        if i >= FLY:
+            need("y", t_ze)
+            need_sem("y", "zs%d" % j, ztot[j])
+            src = T.z[0:32, 0:2048]
+        else:
+            src = T.z[:, 0:512]
+        g.sync.dma_start(T.y[i * rows:(i + 1) * rows, :], src).then_inc(S["zs%d" % j], 16)
+        ztot[j] += 16
+
+    need_sem("v", "lidx", 16)
+    done("v", V.tensor_scalar(T.owni[:], T.idxs[:], 14, None, A.arith_shift_right))
+    t = done("v", V.tensor_scalar(T.loci[:], T.idxs[:], 16383, None, A.bitwise_and))
+    need("v", t)
+    t = done("v", V.tensor_copy(T.ownf[:], T.owni[:]))
+    t_loc = done("v", V.tensor_scalar(T.raw[:, 64:4 * CW:CW], T.loci[:], 1.0, None, A.add))
+    need("v", t, t_io8)
+    for c in range(4):
+        t_oh = done("v", V.tensor_scalar(T.oh8[:, c * 8:(c + 1) * 8], T.io8[:], T.ownf[:, c:c + 1], None, A.is_equal))
+    need("p", t_oh, t_lb)
+    done("p", PE.matmul(T.ppre[:, 0:32], T.lb[:], T.oh8[:, 0:32], True, False))
+    done("p", PE.matmul(T.ppre[:, 8:32], T.onesb[:], T.oh8[:, 0:24], False, False))
+    done("p", PE.matmul(T.ppre[:, 16:32], T.onesb[:], T.oh8[:, 0:16], False, False))
+    t = done("p", PE.matmul(T.ppre[:, 24:32], T.onesb[:], T.oh8[:, 0:8], False, True))
+    need("v", t, t_oh)
+    t = done("v", V.tensor_tensor(T.place[:], T.oh8[:], T.ppre[:, 0:32], A.mult))
+    need("v", t, t_io1)
+
+    order = send_order(rank)
+    mych = chunks(rank)
+    pc = [T.pc0, T.pc1]
+    t_cp = {}
+    need_sem("p", "lgr", 64)
+    nsent = 0
+    for di, d in enumerate(order):
+        tp = []
+        for c in range(4):
+            b = (di * 4 + c) * 128
+            tp.append(done("v", V.tensor_scalar(T.pmat[:, b:b + 128], T.io1[:], T.place[:, c * 8 + d:c * 8 + d + 1],
+                                                None, A.is_equal)))
+        if di >= 2:
+            need("p", t_cp[di - 2])
+        for c in range(4):
+            b = (di * 4 + c) * 128
+            need("p", tp[c], t_loc)
+            t = done("p", PE.matmul(pc[di % 2][:, 0:NB], T.pmat[:, b:b + 128], T.raw[:, c * CW:c * CW + NB],
+                                    c == 0, c == 3))
+        need("s", t)
+        if d == rank:
+            k = mych.index(rank)
+            t_cp[di] = done("s", SC.activation(T.land[:, k * CW:k * CW + NB], pc[di % 2][:, 0:NB], ACT.Copy))
+            t_own = t_cp[di]
+            continue
+        t_cp[di] = done("s", SC.activation(T.sendb[:, di * CW:di * CW + NB], pc[di % 2][:, 0:NB], ACT.Copy))
+        need("g", t_cp[di])
+        if topo.may_write(core, cores[d]):
+            k = chunks(d).index(rank)
+            write(cores[d], T.land[:, k * CW:k * CW + NB], T.sendb[:, di * CW:di * CW + NB], S["arr%d" % rank], S.sent)
+        else:
+            write(forwarder(rank, d), T.fw[:], T.sendb[:, di * CW:di * CW + NB], S.fin, S.sent)
+        nsent += NE
+
+    def arrive(q, P):
+        if mych[P] == rank:
+            need(q, t_own)
+        else:
+            need_sem(q, "arr%d" % mych[P], NE)
+
+    def val(P):
+        return T.land[:, P * CW + 64:P * CW + 65]
+
+    def eqb(P, F):
+        b = (P * (P + 1) // 2 + F) * 128
+        return T.eq[:, b:b + 128]
+
+    pb = [T.pb0, T.pb1]
+    banks = [T.pg0, T.pg1, T.pg2, T.pc0, T.pc1, T.ppre]
+    bank = {6: banks[0], 5: banks[1], 4: banks[2], 7: banks[3], 3: banks[4], 2: banks[5], 1: banks[0], 0: banks[1]}
+    t_E, t_bcc, t_sf, t_conv, t_oc, t_mm = {}, {}, {}, {}, {}, {}
+    need("p", t_cp[N - 2], t_cp[N - 1])
+
+    def v_diag(P):
+        arrive("v", P)
+        need("v", t_id)
+        return done("v", V.tensor_scalar(T.diag[:, P * 128:(P + 1) * 128], T.ident[:], val(P), None, A.mult))
+
+    def p_bc(P, t_d):
+        need("p", t_d)
+        if P >= 2:
+            need("p", t_bcc[P - 2])
+        return done("p", PE.matmul(pb[P % 2][:, 0:128], T.onesf[:], T.diag[:, P * 128:(P + 1) * 128], True, True))
+
+    def s_bcc(P, t_b):
+        need("s", t_b)
+        t_bcc[P] = done("s", SC.activation(T.rowb[:, P * 128:(P + 1) * 128], pb[P % 2][:, 0:128], ACT.Copy))
+
+    def v_E(P, F):
+        need("v", t_bcc[F])
+        t_E[(P, F)] = done("v", V.tensor_scalar(eqb(P, F), T.rowb[:, F * 128:(F + 1) * 128], val(P), None, A.is_equal))
+        if P == F:
+            need("v", t_E[(P, F)], t_mle)
+            t_E[(P, F)] = done("v", V.tensor_tensor(eqb(P, F), eqb(P, F), T.mle[:], A.mult))
+
+    def v_conv(P):
+        need("v", t_sf[P])
+        t_conv[P] = done("v", V.tensor_copy(T.sidx[:, P:P + 1], T.sel[:, P:P + 1]))
+
+    def p_mm(P, F):
+        arrive("p", P)
+        need("p", t_E[(P, F)])
+        t_mm[F] = done("p", PE.matmul(bank[F][:, 0:64], eqb(P, F), T.land[:, P * CW:P * CW + 64], P == F, P == N - 1))
+
+    def s_flag(P):
+        b = (P * (P + 1) // 2) * 128
+        n = (P + 1) * 128
+        need("s", *[t_E[(P, F)] for F in range(P + 1)])
+        t1 = done("s", SC.activation(T.junk[:, b:b + n], T.eq[:, b:b + n], ACT.Copy, accum_out=T.cnt[:, P:P + 1]))
+        need("s", t1)
+        t2 = done("s", SC.activation(T.fl[:, P:P + 1], T.cnt[:, P:P + 1], ACT.Relu, bias=2.0, scale=-1.0))
+        need("s", t2)
+        arrive("s", P)
+        t_sf[P] = done("s", SC.activation(T.sel[:, P:P + 1], T.fl[:, P:P + 1], ACT.Identity, bias=-1.0, scale=val(P)))
+
+    def s_oc(F):
+        need("s", t_mm[F])
+        t_oc[F] = done("s", SC.activation(T.outb[:, F * 64:(F + 1) * 64], bank[F][:, 0:64], ACT.Copy))
+
+    early = [6, 5, 4, 3, 2]
+    L = N - 1
+    for P in range(L):
+        s_bcc(P, p_bc(P, v_diag(P)))
+        for F in range(P - 1, -1, -1):
+            v_E(P, F)
+            if F == P - 1:
+                v_conv(F)
+        v_E(P, P)
+        for F in early:
+            if F < P:
+                p_mm(P, F)
+        if P in early:
+            p_mm(P, P)
+        s_flag(P)
+    t_d = v_diag(L)
+    for F in range(L - 1, -1, -1):
+        v_E(L, F)
+        if F == L - 1:
+            v_conv(F)
+    for F in (6, 5, 4):
+        p_mm(L, F)
+    t_b = p_bc(L, t_d)
+    for F in (3, 2):
+        p_mm(L, F)
+    for F in (6, 5, 4):
+        s_oc(F)
+    s_bcc(L, t_b)
+    v_E(L, L)
+    p_mm(L, L)
+    s_flag(L)
+    for F in (7, 3, 2):
+        s_oc(F)
+    v_conv(L)
+    for F, freed in ((1, 6), (0, 5)):
+        need("p", t_oc[freed])
+        for P in range(F, N):
+            p_mm(P, F)
+        s_oc(F)
+
+    for j in range(FLY):
+        need_sem("g", "zs%d" % j, ztot[j])
+    for F in (6, 5, 4, 7, 3, 2, 1, 0):
+        need("g", t_oc[F], t_conv[F])
+        g.indirect_dma_start(out=T.y[:], out_offset=IndirectOffsetOnAxis(ap=T.sidx[:, F:F + 1], axis=0),
+                             in_=T.outb[:, F * 64:(F + 1) * 64], in_offset=None,
+                             bounds_check=T.y.shape[0] - 1, oob_is_err=False).then_inc(S.sc, 16)
+    g.wait_ge(S.sc, 16 * N)
+    g.wait_ge(S.sent, nsent)
+    for q in ("v", "p", "s", "g"):
+        need("g", (q, num[q]))
+    need_sem("g", "lgr", 64)
+    need_sem("g", "lidx", 16)
+    for s in range(N):
+        if s != rank:
+            need_sem("g", "arr%d" % s, NE)

@@ -1,11 +1,11 @@
-from concourse.bass import IndirectOffsetOnAxis
+from concourse.bass import IndirectOffsetOnAxis, DstId, RemoteDMATransfer
 from concourse.mybir import AluOpType, ActivationFunctionType
 
-P128 = 128
 CW = 68
 NB = 65
 NSL = 16
-FLY = 3
+HEAD = 2
+FLY = 4
 
 SCRATCH = {
     "idxs": ("sbuf", [128, 4], "int32"),
@@ -22,10 +22,9 @@ SCRATCH = {
     "mle": ("sbuf", [128, 128], "float32"),
     "oh8": ("sbuf", [128, 32], "bfloat16"),
     "place": ("sbuf", [128, 32], "float32"),
-    "pmat": ("sbuf", [128, 32 * 128], "float32"),
-    "sendb": ("sbuf", [128, 8 * CW], "float32"),
+    "pmat": ("sbuf", [128, 16 * 128], "float32"),
+    "sendb": ("sbuf", [128, 4 * CW], "float32"),
     "land": ("sbuf", [128, 8 * CW], "float32"),
-    "fw": ("sbuf", [128, NB], "float32"),
     "diag": ("sbuf", [128, 1024], "float32"),
     "rowb": ("sbuf", [128, 1024], "float32"),
     "eq": ("sbuf", [128, 36 * 128], "float32"),
@@ -45,7 +44,7 @@ SCRATCH = {
     "pg1": ("psum", [128, 512], "float32"),
     "pg2": ("psum", [128, 512], "float32"),
 }
-SEMAPHORES = ["sv", "sp", "ss", "sg", "lidx", "lgr", "zs0", "zs1", "zs2", "sent", "fin", "fout", "sc"] + \
+SEMAPHORES = ["sv", "sp", "ss", "sg", "lidx", "lgr", "zs0", "zs1", "zs2", "zs3", "gate", "sent", "fin", "fout", "sc"] + \
              ["arr%d" % s for s in range(8)]
 
 
@@ -66,6 +65,7 @@ def rank_program(g, core, T, topo):
     NE = 8
     A = AluOpType
     ACT = ActivationFunctionType
+    V, PE, SC = g.vector, g.tensor, g.scalar
 
     def split(r):
         me = cores[r]
@@ -73,11 +73,7 @@ def rank_program(g, core, T, topo):
         near = sorted([d for d in range(N) if d != r and topo.may_write(me, cores[d])], key=lambda d: (d - r) % N)
         return far, near
 
-    def send_order(r):
-        far, near = split(r)
-        return far + near + [r]
-
-    def forwarder(r, d):
+    def helper(r, d):
         me = cores[r]
         far, _ = split(r)
         hs = [h for h in range(topo.CORES_PER_CHIP * topo.CHIPS)
@@ -87,27 +83,19 @@ def rank_program(g, core, T, topo):
     def chunks(x):
         est = {}
         for s in range(N):
-            hop = 0.0 if s == x else (3.0 if topo.may_write(cores[s], cores[x]) else 5.5)
-            est[s] = send_order(s).index(x) * 0.9 + hop
+            far, near = split(s)
+            if s == x:
+                est[s] = 0.0
+            elif x in near:
+                est[s] = 1.0 + near.index(x)
+            else:
+                est[s] = 100.0 + far.index(x)
         return sorted(range(N), key=lambda s: (est[s], s))
 
     def write(dst, out_ap, in_ap, rsem, lsem):
         rid, pid, _ = topo.addr(dst)
         g.remote_dma(out_ap=out_ap, in_ap=in_ap, remote_sem=rsem, local_sem=lsem, pid=pid, routing_id=rid,
                      dma_engine_mask=_low(topo.mask(core, dst), NE))
-
-    rank = T.rank_of(core)
-    if rank is None:
-        for r in range(N):
-            if topo.chip(cores[r]) != topo.chip(core):
-                continue
-            for d in split(r)[0]:
-                if forwarder(r, d) == core:
-                    k = chunks(d).index(r)
-                    g.wait_ge(S.fin, NE)
-                    write(cores[d], T.land[:, k * CW:k * CW + NB], T.fw[:], S["arr%d" % r], S.fout)
-                    g.wait_ge(S.fout, NE)
-        return
 
     Q = {"v": g.vector, "p": g.tensor, "s": g.scalar, "g": g, "y": g.sync}
     SQ = {"v": S.sv, "p": S.sp, "s": S.ss, "g": S.sg}
@@ -130,13 +118,67 @@ def rank_program(g, core, T, topo):
             Q[q].wait_ge(S[name], val)
             seen[(q, name)] = val
 
-    V, PE, SC = g.vector, g.tensor, g.scalar
+    def running_count(w, t_in):
+        need("p", t_in)
+        done("p", PE.matmul(T.ppre[:, 0:4 * w], T.lb[:], T.oh8[:, 0:4 * w], True, False))
+        for k in (1, 2, 3):
+            t = done("p", PE.matmul(T.ppre[:, k * w:4 * w], T.onesb[:], T.oh8[:, 0:(4 - k) * w], False, k == 3))
+        need("v", t, t_in)
+        t = done("v", V.tensor_tensor(T.place[:, 0:4 * w], T.oh8[:, 0:4 * w], T.ppre[:, 0:4 * w], A.mult))
+        need("v", t)
+
+    def bucket(di, col, ps, out_ap, before):
+        tp = []
+        for c in range(4):
+            b = (di * 4 + c) * 128
+            tp.append(done("v", V.tensor_scalar(T.pmat[:, b:b + 128], T.io1[:], T.place[:, col(c):col(c) + 1],
+                                                None, A.is_equal)))
+        need("p", *before)
+        for c in range(4):
+            b = (di * 4 + c) * 128
+            need("p", tp[c])
+            t = done("p", PE.matmul(ps[:, 0:NB], T.pmat[:, b:b + 128], T.raw[:, c * CW:c * CW + NB], c == 0, c == 3))
+        need("s", t)
+        return done("s", SC.activation(out_ap, ps[:, 0:NB], ACT.Copy))
+
+    def finish():
+        for q in ("v", "p", "s", "g"):
+            need("g", (q, num[q]))
+
+    rank = T.rank_of(core)
+    if rank is None:
+        jobs = [(r, d) for r in range(N) if topo.chip(cores[r]) == topo.chip(core)
+                for d in split(r)[0] if helper(r, d) == core]
+        for (r, d) in jobs:
+            nin = bin(topo.mask(cores[r], core)).count("1")
+            t_ob = done("v", V.memset(T.onesb[:], 1.0))
+            need("g", t_ob)
+            t_lb = done("g", g.affine_select(T.lb[:], T.onesb[:], [[1, 128]], A.is_ge, 0.0, 0, -1))
+            t_io1 = done("g", g.iota(T.io1[:], [[1, 128]], 1, 0, allow_small_or_imprecise_dtypes=True))
+            need("v", t_io1)
+            need("p", t_lb)
+            need_sem("v", "fin", nin)
+            need_sem("p", "fin", nin)
+            t = done("v", V.tensor_scalar(T.oh8[:, 0:4], T.raw[:, 65:4 * CW:CW], float(d), None, A.is_equal))
+            running_count(1, t)
+            t = bucket(0, lambda c: c, T.pc0, T.sendb[:, 0:NB], [])
+            need("g", t)
+            k = chunks(d).index(r)
+            write(cores[d], T.land[:, k * CW:k * CW + NB], T.sendb[:, 0:NB], S["arr%d" % r], S.fout)
+            g.wait_ge(S.fout, NE)
+            finish()
+        return
+
+    rows = T.y.shape[0] // NSL
+    far, near = split(rank)
 
     g.sync.dma_start(T.idxs[:], T.idx[:]).then_inc(S.lidx, 16)
     for c in range(4):
         SC.dma_start(T.raw[:, c * CW:c * CW + 64], T.gr[c * 128:(c + 1) * 128, :]).then_inc(S.lgr, 16)
     t_z = done("v", V.memset(T.z[:, 0:512], 0.0))
     t_ob = done("v", V.memset(T.onesb[:], 1.0))
+    for c in range(4):
+        t_pad = done("v", V.memset(T.raw[:, c * CW + 64:(c + 1) * CW], 0.0))
     t_of = done("v", V.memset(T.onesf[:], 1.0))
     need("s", t_z)
     for k in range(1, 4):
@@ -145,74 +187,66 @@ def rank_program(g, core, T, topo):
     need("g", t_ob)
     t_lb = done("g", g.affine_select(T.lb[:], T.onesb[:], [[1, 128]], A.is_ge, 0.0, 0, -1))
     t_io1 = done("g", g.iota(T.io1[:], [[1, 128]], 1, 0, allow_small_or_imprecise_dtypes=True))
-    need("g", t_of)
-    t_id = done("g", g.affine_select(T.ident[:], T.onesf[:], [[-1, 128]], A.is_equal, 0.0, 0, 1))
-    t_mle = done("g", g.affine_select(T.mle[:], T.onesf[:], [[-1, 128]], A.is_ge, 0.0, 0, 1))
 
-    rows = T.y.shape[0] // NSL
     ztot = [0] * FLY
     need("y", t_z)
     for i in range(NSL):
         j = i % FLY
-        if i >= FLY:
+        if i >= HEAD:
             need("y", t_ze)
+            need_sem("y", "gate", 1)
+        if i >= FLY:
             need_sem("y", "zs%d" % j, ztot[j])
-            src = T.z[0:32, 0:2048]
-        else:
-            src = T.z[:, 0:512]
-        g.sync.dma_start(T.y[i * rows:(i + 1) * rows, :], src).then_inc(S["zs%d" % j], 16)
+        g.sync.dma_start(T.y[i * rows:(i + 1) * rows, :], T.z[:, 0:512] if i < HEAD else T.z[0:32, 0:2048]) \
+            .then_inc(S["zs%d" % j], 16)
         ztot[j] += 16
 
     need_sem("v", "lidx", 16)
     done("v", V.tensor_scalar(T.owni[:], T.idxs[:], 14, None, A.arith_shift_right))
     t = done("v", V.tensor_scalar(T.loci[:], T.idxs[:], 16383, None, A.bitwise_and))
-    need("v", t)
+    need("v", t, t_pad)
     t = done("v", V.tensor_copy(T.ownf[:], T.owni[:]))
+    done("v", V.tensor_copy(T.raw[:, 65:4 * CW:CW], T.owni[:]))
     t_loc = done("v", V.tensor_scalar(T.raw[:, 64:4 * CW:CW], T.loci[:], 1.0, None, A.add))
     need("v", t, t_io8)
     for c in range(4):
         t_oh = done("v", V.tensor_scalar(T.oh8[:, c * 8:(c + 1) * 8], T.io8[:], T.ownf[:, c:c + 1], None, A.is_equal))
-    need("p", t_oh, t_lb)
-    done("p", PE.matmul(T.ppre[:, 0:32], T.lb[:], T.oh8[:, 0:32], True, False))
-    done("p", PE.matmul(T.ppre[:, 8:32], T.onesb[:], T.oh8[:, 0:24], False, False))
-    done("p", PE.matmul(T.ppre[:, 16:32], T.onesb[:], T.oh8[:, 0:16], False, False))
-    t = done("p", PE.matmul(T.ppre[:, 24:32], T.onesb[:], T.oh8[:, 0:8], False, True))
-    need("v", t, t_oh)
-    t = done("v", V.tensor_tensor(T.place[:], T.oh8[:], T.ppre[:, 0:32], A.mult))
-    need("v", t, t_io1)
 
-    order = send_order(rank)
+    hs = [helper(rank, d) for d in far]
+    m = topo.mask(core, hs[0])
+    for h in hs:
+        m &= topo.mask(core, h)
+    need("g", t_loc)
+    need_sem("g", "lgr", 64)
+    g.remote_dma_fused([RemoteDMATransfer(dst_ids=[DstId(rid=topo.addr(h)[0], pnc=topo.addr(h)[1]) for h in hs],
+                                          dma_engine_mask=m, remote_sem=S.fin, srcs=[T.raw[:]],
+                                          dsts=[T.raw[:] for h in hs], alu_op=0)], local_sem=S.sent)
+    g.sem_inc(S.gate, 1)
+    nsent = bin(m).count("1")
+    need("g", t_of)
+    t_id = done("g", g.affine_select(T.ident[:], T.onesf[:], [[-1, 128]], A.is_equal, 0.0, 0, 1))
+    t_mle = done("g", g.affine_select(T.mle[:], T.onesf[:], [[-1, 128]], A.is_ge, 0.0, 0, 1))
+
+    need("p", t_lb)
+    running_count(8, t_oh)
+    need("v", t_io1)
+
     mych = chunks(rank)
     pc = [T.pc0, T.pc1]
     t_cp = {}
     need_sem("p", "lgr", 64)
-    nsent = 0
-    for di, d in enumerate(order):
-        tp = []
-        for c in range(4):
-            b = (di * 4 + c) * 128
-            tp.append(done("v", V.tensor_scalar(T.pmat[:, b:b + 128], T.io1[:], T.place[:, c * 8 + d:c * 8 + d + 1],
-                                                None, A.is_equal)))
-        if di >= 2:
-            need("p", t_cp[di - 2])
-        for c in range(4):
-            b = (di * 4 + c) * 128
-            need("p", tp[c], t_loc)
-            t = done("p", PE.matmul(pc[di % 2][:, 0:NB], T.pmat[:, b:b + 128], T.raw[:, c * CW:c * CW + NB],
-                                    c == 0, c == 3))
-        need("s", t)
+    need("p", t_loc)
+    for di, d in enumerate(near + [rank]):
+        before = [t_cp[di - 2]] if di >= 2 else []
         if d == rank:
             k = mych.index(rank)
-            t_cp[di] = done("s", SC.activation(T.land[:, k * CW:k * CW + NB], pc[di % 2][:, 0:NB], ACT.Copy))
+            t_cp[di] = bucket(di, lambda c: c * 8 + d, pc[di % 2], T.land[:, k * CW:k * CW + NB], before)
             t_own = t_cp[di]
             continue
-        t_cp[di] = done("s", SC.activation(T.sendb[:, di * CW:di * CW + NB], pc[di % 2][:, 0:NB], ACT.Copy))
+        t_cp[di] = bucket(di, lambda c: c * 8 + d, pc[di % 2], T.sendb[:, di * CW:di * CW + NB], before)
         need("g", t_cp[di])
-        if topo.may_write(core, cores[d]):
-            k = chunks(d).index(rank)
-            write(cores[d], T.land[:, k * CW:k * CW + NB], T.sendb[:, di * CW:di * CW + NB], S["arr%d" % rank], S.sent)
-        else:
-            write(forwarder(rank, d), T.fw[:], T.sendb[:, di * CW:di * CW + NB], S.fin, S.sent)
+        k = chunks(d).index(rank)
+        write(cores[d], T.land[:, k * CW:k * CW + NB], T.sendb[:, di * CW:di * CW + NB], S["arr%d" % rank], S.sent)
         nsent += NE
 
     def arrive(q, P):
@@ -229,10 +263,9 @@ def rank_program(g, core, T, topo):
         return T.eq[:, b:b + 128]
 
     pb = [T.pb0, T.pb1]
-    banks = [T.pg0, T.pg1, T.pg2, T.pc0, T.pc1, T.ppre]
-    bank = {6: banks[0], 5: banks[1], 4: banks[2], 7: banks[3], 3: banks[4], 2: banks[5], 1: banks[0], 0: banks[1]}
+    bank = {0: T.pg0, 1: T.pg1, 2: T.pg2, 3: T.pc0, 4: T.pc1, 5: T.ppre, 6: T.pc0, 7: T.pg2}
     t_E, t_bcc, t_sf, t_conv, t_oc, t_mm = {}, {}, {}, {}, {}, {}
-    need("p", t_cp[N - 2], t_cp[N - 1])
+    need("p", *[t_cp[k] for k in t_cp])
 
     def v_diag(P):
         arrive("v", P)
@@ -250,6 +283,7 @@ def rank_program(g, core, T, topo):
         t_bcc[P] = done("s", SC.activation(T.rowb[:, P * 128:(P + 1) * 128], pb[P % 2][:, 0:128], ACT.Copy))
 
     def v_E(P, F):
+        arrive("v", P)
         need("v", t_bcc[F])
         t_E[(P, F)] = done("v", V.tensor_scalar(eqb(P, F), T.rowb[:, F * 128:(F + 1) * 128], val(P), None, A.is_equal))
         if P == F:
@@ -280,58 +314,53 @@ def rank_program(g, core, T, topo):
         need("s", t_mm[F])
         t_oc[F] = done("s", SC.activation(T.outb[:, F * 64:(F + 1) * 64], bank[F][:, 0:64], ACT.Copy))
 
-    early = [6, 5, 4, 3, 2]
-    L = N - 1
-    for P in range(L):
+    H = N - len(far)
+    for P in range(H):
         s_bcc(P, p_bc(P, v_diag(P)))
         for F in range(P - 1, -1, -1):
             v_E(P, F)
             if F == P - 1:
                 v_conv(F)
         v_E(P, P)
-        for F in early:
-            if F < P:
-                p_mm(P, F)
-        if P in early:
-            p_mm(P, P)
+        for F in range(P + 1):
+            p_mm(P, F)
         s_flag(P)
-    t_d = v_diag(L)
-    for F in range(L - 1, -1, -1):
-        v_E(L, F)
-        if F == L - 1:
+    t_dg = {}
+    for F in range(H - 1, -1, -1):
+        for P in range(H, N):
+            v_E(P, F)
+        if F == H - 1:
             v_conv(F)
-    for F in (6, 5, 4):
-        p_mm(L, F)
-    t_b = p_bc(L, t_d)
-    for F in (3, 2):
-        p_mm(L, F)
-    for F in (6, 5, 4):
+            for P in range(H, N):
+                t_dg[P] = v_diag(P)
+        for P in range(H, N):
+            p_mm(P, F)
         s_oc(F)
-    s_bcc(L, t_b)
-    v_E(L, L)
-    p_mm(L, L)
-    s_flag(L)
-    for F in (7, 3, 2):
-        s_oc(F)
-    v_conv(L)
-    for F, freed in ((1, 6), (0, 5)):
-        need("p", t_oc[freed])
+    for P in range(H, N):
+        s_bcc(P, p_bc(P, t_dg[P]))
+    for P in range(H, N):
+        for F in range(H, P + 1):
+            v_E(P, F)
+    freed = {6: 3, 7: 2}
+    for F in range(H, N):
+        s_flag(F)
+        v_conv(F)
+        if F in freed:
+            need("p", t_oc[freed[F]])
         for P in range(F, N):
             p_mm(P, F)
         s_oc(F)
 
     for j in range(FLY):
         need_sem("g", "zs%d" % j, ztot[j])
-    for F in (6, 5, 4, 7, 3, 2, 1, 0):
+    for F in list(range(H - 1, -1, -1)) + list(range(H, N)):
         need("g", t_oc[F], t_conv[F])
         g.indirect_dma_start(out=T.y[:], out_offset=IndirectOffsetOnAxis(ap=T.sidx[:, F:F + 1], axis=0),
                              in_=T.outb[:, F * 64:(F + 1) * 64], in_offset=None,
                              bounds_check=T.y.shape[0] - 1, oob_is_err=False).then_inc(S.sc, 16)
     g.wait_ge(S.sc, 16 * N)
     g.wait_ge(S.sent, nsent)
-    for q in ("v", "p", "s", "g"):
-        need("g", (q, num[q]))
-    need_sem("g", "lgr", 64)
+    finish()
     need_sem("g", "lidx", 16)
     for s in range(N):
         if s != rank:

@@ -4,14 +4,17 @@ from concourse.mybir import AluOpType, ActivationFunctionType
 CW = 68
 NB = 65
 NSL = 16
-HEAD = 2
+HEAD = 3
 FLY = 4
+BIG = 32768.0
 
 SCRATCH = {
     "idxs": ("sbuf", [128, 4], "int32"),
     "owni": ("sbuf", [128, 4], "int32"),
     "loci": ("sbuf", [128, 4], "int32"),
     "ownf": ("sbuf", [128, 4], "float32"),
+    "locf": ("sbuf", [128, 4], "float32"),
+    "numb": ("sbuf", [128, 4], "float32"),
     "raw": ("sbuf", [128, 4 * CW], "float32"),
     "io8": ("sbuf", [128, 8], "float32"),
     "io1": ("sbuf", [128, 128], "float32"),
@@ -19,7 +22,7 @@ SCRATCH = {
     "onesb": ("sbuf", [128, 128], "bfloat16"),
     "lb": ("sbuf", [128, 128], "bfloat16"),
     "ident": ("sbuf", [128, 128], "float32"),
-    "mle": ("sbuf", [128, 128], "float32"),
+    "mge": ("sbuf", [128, 128], "float32"),
     "oh8": ("sbuf", [128, 32], "bfloat16"),
     "place": ("sbuf", [128, 32], "float32"),
     "pmat": ("sbuf", [128, 16 * 128], "float32"),
@@ -30,8 +33,7 @@ SCRATCH = {
     "eq": ("sbuf", [128, 36 * 128], "float32"),
     "junk": ("sbuf", [128, 36 * 128], "float32"),
     "cnt": ("sbuf", [128, 8], "float32"),
-    "fl": ("sbuf", [128, 8], "float32"),
-    "sel": ("sbuf", [128, 8], "float32"),
+    "vm": ("sbuf", [128, 8], "float32"),
     "sidx": ("sbuf", [128, 8], "int32"),
     "outb": ("sbuf", [128, 512], "float32"),
     "z": ("sbuf", [128, 2048], "float32"),
@@ -44,8 +46,8 @@ SCRATCH = {
     "pg1": ("psum", [128, 512], "float32"),
     "pg2": ("psum", [128, 512], "float32"),
 }
-SEMAPHORES = ["sv", "sp", "ss", "sg", "lidx", "lgr", "zs0", "zs1", "zs2", "zs3", "gate", "sent", "fin", "fout", "sc"] + \
-             ["arr%d" % s for s in range(8)]
+SEMAPHORES = ["sv", "sp", "ss", "sg", "lidx", "lgr", "zs0", "zs1", "zs2", "zs3", "gate", "sent", "fin0", "fin", "fout",
+              "sc"] + ["arr%d" % s for s in range(8)] + ["arn%d" % s for s in range(8)]
 
 
 def _low(mask, n):
@@ -97,6 +99,15 @@ def rank_program(g, core, T, topo):
         g.remote_dma(out_ap=out_ap, in_ap=in_ap, remote_sem=rsem, local_sem=lsem, pid=pid, routing_id=rid,
                      dma_engine_mask=_low(topo.mask(core, dst), NE))
 
+    def fan(dsts, buf, rsem, lsem):
+        m = topo.mask(core, dsts[0])
+        for h in dsts:
+            m &= topo.mask(core, h)
+        g.remote_dma_fused([RemoteDMATransfer(dst_ids=[DstId(rid=topo.addr(h)[0], pnc=topo.addr(h)[1]) for h in dsts],
+                                              dma_engine_mask=m, remote_sem=rsem, srcs=[buf[:]],
+                                              dsts=[buf[:] for h in dsts], alu_op=0)], local_sem=lsem)
+        return bin(m).count("1")
+
     Q = {"v": g.vector, "p": g.tensor, "s": g.scalar, "g": g, "y": g.sync}
     SQ = {"v": S.sv, "p": S.sp, "s": S.ss, "g": S.sg}
     num = {"v": 0, "p": 0, "s": 0, "g": 0}
@@ -127,19 +138,22 @@ def rank_program(g, core, T, topo):
         t = done("v", V.tensor_tensor(T.place[:, 0:4 * w], T.oh8[:, 0:4 * w], T.ppre[:, 0:4 * w], A.mult))
         need("v", t)
 
-    def bucket(di, col, ps, out_ap, before):
+    def pmats(di, col):
         tp = []
         for c in range(4):
             b = (di * 4 + c) * 128
             tp.append(done("v", V.tensor_scalar(T.pmat[:, b:b + 128], T.io1[:], T.place[:, col(c):col(c) + 1],
                                                 None, A.is_equal)))
+        return tp
+
+    def collect(di, tp, ps, n, rhs, out_ap, before):
         need("p", *before)
         for c in range(4):
             b = (di * 4 + c) * 128
             need("p", tp[c])
-            t = done("p", PE.matmul(ps[:, 0:NB], T.pmat[:, b:b + 128], T.raw[:, c * CW:c * CW + NB], c == 0, c == 3))
+            t = done("p", PE.matmul(ps[:, 0:n], T.pmat[:, b:b + 128], rhs(c), c == 0, c == 3))
         need("s", t)
-        return done("s", SC.activation(out_ap, ps[:, 0:NB], ACT.Copy))
+        return done("s", SC.activation(out_ap, ps[:, 0:n], ACT.Copy))
 
     def finish():
         for q in ("v", "p", "s", "g"):
@@ -150,22 +164,38 @@ def rank_program(g, core, T, topo):
         jobs = [(r, d) for r in range(N) if topo.chip(cores[r]) == topo.chip(core)
                 for d in split(r)[0] if helper(r, d) == core]
         for (r, d) in jobs:
-            nin = bin(topo.mask(cores[r], core)).count("1")
+            hs = [helper(r, x) for x in split(r)[0]]
+            src = cores[r] if core == hs[0] else hs[0]
+            nin0 = bin(topo.mask(cores[r], core)).count("1")
+            nin = bin(topo.mask(src, core)).count("1")
+            k = chunks(d).index(r)
             t_ob = done("v", V.memset(T.onesb[:], 1.0))
             need("g", t_ob)
             t_lb = done("g", g.affine_select(T.lb[:], T.onesb[:], [[1, 128]], A.is_ge, 0.0, 0, -1))
             t_io1 = done("g", g.iota(T.io1[:], [[1, 128]], 1, 0, allow_small_or_imprecise_dtypes=True))
             need("v", t_io1)
             need("p", t_lb)
-            need_sem("v", "fin", nin)
-            need_sem("p", "fin", nin)
-            t = done("v", V.tensor_scalar(T.oh8[:, 0:4], T.raw[:, 65:4 * CW:CW], float(d), None, A.is_equal))
+            need_sem("v", "fin0", nin0)
+            done("v", V.tensor_scalar(T.owni[:], T.idxs[:], 14, None, A.arith_shift_right))
+            t = done("v", V.tensor_scalar(T.loci[:], T.idxs[:], 16383, None, A.bitwise_and))
+            need("v", t)
+            t = done("v", V.tensor_scalar(T.oh8[:, 0:4], T.owni[:], float(d), None, A.is_equal))
+            t_lf = done("v", V.tensor_scalar(T.locf[:], T.loci[:], 1.0, None, A.add))
             running_count(1, t)
-            t = bucket(0, lambda c: c, T.pc0, T.sendb[:, 0:NB], [])
+            tp = pmats(0, lambda c: c)
+            t = collect(0, tp, T.pc1, 1, lambda c: T.locf[:, c:c + 1], T.numb[:, 0:1], [t_lf])
             need("g", t)
-            k = chunks(d).index(r)
-            write(cores[d], T.land[:, k * CW:k * CW + NB], T.sendb[:, 0:NB], S["arr%d" % r], S.fout)
-            g.wait_ge(S.fout, NE)
+            write(cores[d], T.land[:, k * CW + 64:k * CW + 65], T.numb[:, 0:1], S["arn%d" % r], S.fout)
+            nout = NE
+            if core == hs[0] and len(hs) > 1:
+                need_sem("g", "fin", nin)
+                nout += fan(hs[1:], T.raw, S.fin, S.fout)
+            need_sem("p", "fin", nin)
+            t = collect(0, tp, T.pc0, 64, lambda c: T.raw[:, c * CW:c * CW + 64], T.sendb[:, 0:64], [])
+            need("g", t)
+            write(cores[d], T.land[:, k * CW:k * CW + 64], T.sendb[:, 0:64], S["arr%d" % r], S.fout)
+            nout += NE
+            g.wait_ge(S.fout, nout)
             finish()
         return
 
@@ -186,7 +216,6 @@ def rank_program(g, core, T, topo):
     t_io8 = done("g", g.iota(T.io8[:], [[1, 8]], 0, 0, allow_small_or_imprecise_dtypes=True))
     need("g", t_ob)
     t_lb = done("g", g.affine_select(T.lb[:], T.onesb[:], [[1, 128]], A.is_ge, 0.0, 0, -1))
-    t_io1 = done("g", g.iota(T.io1[:], [[1, 128]], 1, 0, allow_small_or_imprecise_dtypes=True))
 
     ztot = [0] * FLY
     need("y", t_z)
@@ -201,31 +230,28 @@ def rank_program(g, core, T, topo):
             .then_inc(S["zs%d" % j], 16)
         ztot[j] += 16
 
+    hs = [helper(rank, d) for d in far]
+    need_sem("g", "lidx", 16)
+    nsent = fan(hs, T.idxs, S.fin0, S.sent)
+    t_io1 = done("g", g.iota(T.io1[:], [[1, 128]], 1, 0, allow_small_or_imprecise_dtypes=True))
+
     need_sem("v", "lidx", 16)
     done("v", V.tensor_scalar(T.owni[:], T.idxs[:], 14, None, A.arith_shift_right))
     t = done("v", V.tensor_scalar(T.loci[:], T.idxs[:], 16383, None, A.bitwise_and))
     need("v", t, t_pad)
     t = done("v", V.tensor_copy(T.ownf[:], T.owni[:]))
-    done("v", V.tensor_copy(T.raw[:, 65:4 * CW:CW], T.owni[:]))
     t_loc = done("v", V.tensor_scalar(T.raw[:, 64:4 * CW:CW], T.loci[:], 1.0, None, A.add))
     need("v", t, t_io8)
     for c in range(4):
         t_oh = done("v", V.tensor_scalar(T.oh8[:, c * 8:(c + 1) * 8], T.io8[:], T.ownf[:, c:c + 1], None, A.is_equal))
 
-    hs = [helper(rank, d) for d in far]
-    m = topo.mask(core, hs[0])
-    for h in hs:
-        m &= topo.mask(core, h)
     need("g", t_loc)
     need_sem("g", "lgr", 64)
-    g.remote_dma_fused([RemoteDMATransfer(dst_ids=[DstId(rid=topo.addr(h)[0], pnc=topo.addr(h)[1]) for h in hs],
-                                          dma_engine_mask=m, remote_sem=S.fin, srcs=[T.raw[:]],
-                                          dsts=[T.raw[:] for h in hs], alu_op=0)], local_sem=S.sent)
+    nsent += fan(hs[0:1], T.raw, S.fin, S.sent)
     g.sem_inc(S.gate, 1)
-    nsent = bin(m).count("1")
     need("g", t_of)
     t_id = done("g", g.affine_select(T.ident[:], T.onesf[:], [[-1, 128]], A.is_equal, 0.0, 0, 1))
-    t_mle = done("g", g.affine_select(T.mle[:], T.onesf[:], [[-1, 128]], A.is_ge, 0.0, 0, 1))
+    t_mge = done("g", g.affine_select(T.mge[:], T.onesf[:], [[1, 128]], A.is_ge, 0.0, 0, -1))
 
     need("p", t_lb)
     running_count(8, t_oh)
@@ -236,41 +262,53 @@ def rank_program(g, core, T, topo):
     t_cp = {}
     need_sem("p", "lgr", 64)
     need("p", t_loc)
+
+    def rawc(c):
+        return T.raw[:, c * CW:c * CW + NB]
+
     for di, d in enumerate(near + [rank]):
         before = [t_cp[di - 2]] if di >= 2 else []
+        tp = pmats(di, lambda c: c * 8 + d)
         if d == rank:
             k = mych.index(rank)
-            t_cp[di] = bucket(di, lambda c: c * 8 + d, pc[di % 2], T.land[:, k * CW:k * CW + NB], before)
+            t_cp[di] = collect(di, tp, pc[di % 2], NB, rawc, T.land[:, k * CW:k * CW + NB], before)
             t_own = t_cp[di]
             continue
-        t_cp[di] = bucket(di, lambda c: c * 8 + d, pc[di % 2], T.sendb[:, di * CW:di * CW + NB], before)
+        t_cp[di] = collect(di, tp, pc[di % 2], NB, rawc, T.sendb[:, di * CW:di * CW + NB], before)
         need("g", t_cp[di])
         k = chunks(d).index(rank)
         write(cores[d], T.land[:, k * CW:k * CW + NB], T.sendb[:, di * CW:di * CW + NB], S["arr%d" % rank], S.sent)
         nsent += NE
 
-    def arrive(q, P):
+    H = N - len(far)
+
+    def arrive(q, P, what):
         if mych[P] == rank:
             need(q, t_own)
-        else:
+        elif P < H or what == "data":
             need_sem(q, "arr%d" % mych[P], NE)
+        else:
+            need_sem(q, "arn%d" % mych[P], NE)
 
     def val(P):
         return T.land[:, P * CW + 64:P * CW + 65]
 
+    def blk(P, F):
+        return (P * N - P * (P - 1) // 2 + F - P) * 128
+
     def eqb(P, F):
-        b = (P * (P + 1) // 2 + F) * 128
-        return T.eq[:, b:b + 128]
+        return T.eq[:, blk(P, F):blk(P, F) + 128]
 
     pb = [T.pb0, T.pb1]
-    bank = {0: T.pg0, 1: T.pg1, 2: T.pg2, 3: T.pc0, 4: T.pc1, 5: T.ppre, 6: T.pc0, 7: T.pg2}
-    t_E, t_bcc, t_sf, t_conv, t_oc, t_mm = {}, {}, {}, {}, {}, {}
-    need("p", *[t_cp[k] for k in t_cp])
+    bank = [T.pg0, T.pg1, T.pg2, T.ppre, T.pc0, T.pc1, T.pb0, T.pb1]
+    t_E, t_bcc, t_vm, t_cnt, t_idx, t_oc, t_mm = {}, {}, {}, {}, {}, {}, {}
 
     def v_diag(P):
-        arrive("v", P)
+        arrive("v", P, "numbers")
         need("v", t_id)
-        return done("v", V.tensor_scalar(T.diag[:, P * 128:(P + 1) * 128], T.ident[:], val(P), None, A.mult))
+        t = done("v", V.tensor_scalar(T.diag[:, P * 128:(P + 1) * 128], T.ident[:], val(P), None, A.mult))
+        t_vm[P] = done("v", V.tensor_scalar(T.vm[:, P:P + 1], val(P), -(1.0 + BIG), None, A.add))
+        return t
 
     def p_bc(P, t_d):
         need("p", t_d)
@@ -283,85 +321,78 @@ def rank_program(g, core, T, topo):
         t_bcc[P] = done("s", SC.activation(T.rowb[:, P * 128:(P + 1) * 128], pb[P % 2][:, 0:128], ACT.Copy))
 
     def v_E(P, F):
-        arrive("v", P)
+        arrive("v", P, "numbers")
         need("v", t_bcc[F])
         t_E[(P, F)] = done("v", V.tensor_scalar(eqb(P, F), T.rowb[:, F * 128:(F + 1) * 128], val(P), None, A.is_equal))
         if P == F:
-            need("v", t_E[(P, F)], t_mle)
-            t_E[(P, F)] = done("v", V.tensor_tensor(eqb(P, F), eqb(P, F), T.mle[:], A.mult))
+            need("v", t_E[(P, F)], t_mge)
+            t_E[(P, F)] = done("v", V.tensor_tensor(eqb(P, F), eqb(P, F), T.mge[:], A.mult))
 
-    def v_conv(P):
-        need("v", t_sf[P])
-        t_conv[P] = done("v", V.tensor_copy(T.sidx[:, P:P + 1], T.sel[:, P:P + 1]))
+    def s_cnt(P, F1):
+        b, n = blk(P, P), (F1 - P + 1) * 128
+        need("s", *[t_E[(P, F)] for F in range(P, F1 + 1)])
+        t_cnt[P] = done("s", SC.activation(T.junk[:, b:b + n], T.eq[:, b:b + n], ACT.Copy,
+                                           accum_out=T.cnt[:, P:P + 1]))
+
+    def v_idx(P):
+        need("v", t_cnt[P], t_vm[P])
+        t_idx[P] = done("v", V.tensor_scalar(T.sidx[:, P:P + 1], T.cnt[:, P:P + 1], BIG, T.vm[:, P:P + 1],
+                                             A.mult, A.add))
 
     def p_mm(P, F):
-        arrive("p", P)
+        arrive("p", P, "data")
         need("p", t_E[(P, F)])
-        t_mm[F] = done("p", PE.matmul(bank[F][:, 0:64], eqb(P, F), T.land[:, P * CW:P * CW + 64], P == F, P == N - 1))
-
-    def s_flag(P):
-        b = (P * (P + 1) // 2) * 128
-        n = (P + 1) * 128
-        need("s", *[t_E[(P, F)] for F in range(P + 1)])
-        t1 = done("s", SC.activation(T.junk[:, b:b + n], T.eq[:, b:b + n], ACT.Copy, accum_out=T.cnt[:, P:P + 1]))
-        need("s", t1)
-        t2 = done("s", SC.activation(T.fl[:, P:P + 1], T.cnt[:, P:P + 1], ACT.Relu, bias=2.0, scale=-1.0))
-        need("s", t2)
-        arrive("s", P)
-        t_sf[P] = done("s", SC.activation(T.sel[:, P:P + 1], T.fl[:, P:P + 1], ACT.Identity, bias=-1.0, scale=val(P)))
+        if F >= N - 2:
+            need("p", t_bcc[N - 2], t_bcc[N - 1])
+        t_mm[F] = done("p", PE.matmul(bank[F][:, 0:64], eqb(P, F), T.land[:, P * CW:P * CW + 64], P == 0, P == F))
 
     def s_oc(F):
         need("s", t_mm[F])
         t_oc[F] = done("s", SC.activation(T.outb[:, F * 64:(F + 1) * 64], bank[F][:, 0:64], ACT.Copy))
 
-    H = N - len(far)
-    for P in range(H):
-        s_bcc(P, p_bc(P, v_diag(P)))
-        for F in range(P - 1, -1, -1):
-            v_E(P, F)
-            if F == P - 1:
-                v_conv(F)
-        v_E(P, P)
-        for F in range(P + 1):
-            p_mm(P, F)
-        s_flag(P)
-    t_dg = {}
-    for F in range(H - 1, -1, -1):
-        for P in range(H, N):
-            v_E(P, F)
-        if F == H - 1:
-            v_conv(F)
-            for P in range(H, N):
-                t_dg[P] = v_diag(P)
-        for P in range(H, N):
+    def blocks(F0, F1):
+        t_dg = {F0: v_diag(F0)}
+        for F in range(F0, F1):
+            s_bcc(F, p_bc(F, t_dg[F]))
+            if F + 1 < F1:
+                t_dg[F + 1] = v_diag(F + 1)
+            for P in range(F + 1):
+                v_E(P, F)
+
+    need("p", *[t_cp[k] for k in t_cp])
+    blocks(0, H)
+    for F in range(H):
+        s_cnt(F, H - 1)
+        v_idx(F)
+        for P in range(F + 1):
             p_mm(P, F)
         s_oc(F)
-    for P in range(H, N):
-        s_bcc(P, p_bc(P, t_dg[P]))
-    for P in range(H, N):
-        for F in range(H, P + 1):
-            v_E(P, F)
-    freed = {6: 3, 7: 2}
+    blocks(H, N)
     for F in range(H, N):
-        s_flag(F)
-        v_conv(F)
-        if F in freed:
-            need("p", t_oc[freed[F]])
-        for P in range(F, N):
+        s_cnt(F, N - 1)
+        v_idx(F)
+    for F in range(H, N):
+        for P in range(H):
+            p_mm(P, F)
+    for F in range(H, N):
+        for P in range(H, F + 1):
             p_mm(P, F)
         s_oc(F)
 
     for j in range(FLY):
         need_sem("g", "zs%d" % j, ztot[j])
-    for F in list(range(H - 1, -1, -1)) + list(range(H, N)):
-        need("g", t_oc[F], t_conv[F])
+    for F in range(N):
+        if F == H:
+            g.wait_ge(S.sc, 16 * H)
+        need("g", t_oc[F], t_idx[F])
         g.indirect_dma_start(out=T.y[:], out_offset=IndirectOffsetOnAxis(ap=T.sidx[:, F:F + 1], axis=0),
                              in_=T.outb[:, F * 64:(F + 1) * 64], in_offset=None,
                              bounds_check=T.y.shape[0] - 1, oob_is_err=False).then_inc(S.sc, 16)
     g.wait_ge(S.sc, 16 * N)
     g.wait_ge(S.sent, nsent)
     finish()
-    need_sem("g", "lidx", 16)
     for s in range(N):
         if s != rank:
             need_sem("g", "arr%d" % s, NE)
+        if s in far:
+            need_sem("g", "arn%d" % s, NE)

@@ -47,7 +47,7 @@ SCRATCH = {
     "pg2": ("psum", [128, 512], "float32"),
 }
 SEMAPHORES = ["sv", "sp", "ss", "sg", "lidx", "lgr", "zs0", "zs1", "zs2", "zs3", "gate", "sent", "fin0", "fin", "fout",
-              "sc"] + ["arr%d" % s for s in range(8)] + ["arn%d" % s for s in range(8)]
+              "se", "sc", "sd"] + ["arr%d" % s for s in range(8)] + ["arn%d" % s for s in range(8)]
 
 
 def _low(mask, n):
@@ -321,6 +321,8 @@ def rank_program(g, core, T, topo):
         t_bcc[P] = done("s", SC.activation(T.rowb[:, P * 128:(P + 1) * 128], pb[P % 2][:, 0:128], ACT.Copy))
 
     def v_E(P, F):
+        if (P, F) in t_E:
+            return
         arrive("v", P, "numbers")
         need("v", t_bcc[F])
         t_E[(P, F)] = done("v", V.tensor_scalar(eqb(P, F), T.rowb[:, F * 128:(F + 1) * 128], val(P), None, A.is_equal))
@@ -339,56 +341,73 @@ def rank_program(g, core, T, topo):
         t_idx[P] = done("v", V.tensor_scalar(T.sidx[:, P:P + 1], T.cnt[:, P:P + 1], BIG, T.vm[:, P:P + 1],
                                              A.mult, A.add))
 
-    def p_mm(P, F):
-        arrive("p", P, "data")
-        need("p", t_E[(P, F)])
-        if F >= N - 2:
-            need("p", t_bcc[N - 2], t_bcc[N - 1])
-        t_mm[F] = done("p", PE.matmul(bank[F][:, 0:64], eqb(P, F), T.land[:, P * CW:P * CW + 64], P == 0, P == F))
-
-    def s_oc(F):
-        need("s", t_mm[F])
+    def total(F):
+        for P in range(F + 1):
+            arrive("p", P, "data")
+            need("p", t_E[(P, F)])
+            if F >= N - 2:
+                need("p", t_bcc[N - 2], t_bcc[N - 1])
+            t = done("p", PE.matmul(bank[F][:, 0:64], eqb(P, F), T.land[:, P * CW:P * CW + 64], P == 0, P == F))
+        need("s", t)
         t_oc[F] = done("s", SC.activation(T.outb[:, F * 64:(F + 1) * 64], bank[F][:, 0:64], ACT.Copy))
 
-    def blocks(F0, F1):
-        t_dg = {F0: v_diag(F0)}
-        for F in range(F0, F1):
-            s_bcc(F, p_bc(F, t_dg[F]))
-            if F + 1 < F1:
-                t_dg[F + 1] = v_diag(F + 1)
-            for P in range(F + 1):
-                v_E(P, F)
-
     need("p", *[t_cp[k] for k in t_cp])
-    blocks(0, H)
-    for F in range(H):
-        s_cnt(F, H - 1)
-        v_idx(F)
+    t_dg = {0: v_diag(0)}
+    for F in range(H - 1):
+        s_bcc(F, p_bc(F, t_dg[F]))
+        if F + 1 < H - 1:
+            t_dg[F + 1] = v_diag(F + 1)
         for P in range(F + 1):
-            p_mm(P, F)
-        s_oc(F)
-    blocks(H, N)
+            v_E(P, F)
+    s_cnt(0, H - 2)
+    v_idx(0)
+    total(0)
+    s_bcc(H - 1, p_bc(H - 1, v_diag(H - 1)))
+    for P in range(H):
+        v_E(P, H - 1)
+    for F in range(1, H):
+        if F < H - 1:
+            s_cnt(F, H - 1)
+            v_idx(F)
+        total(F)
     for F in range(H, N):
-        s_cnt(F, N - 1)
-        v_idx(F)
+        t_dg[F] = v_diag(F)
     for F in range(H, N):
-        for P in range(H):
-            p_mm(P, F)
-    for F in range(H, N):
-        for P in range(H, F + 1):
-            p_mm(P, F)
-        s_oc(F)
+        s_bcc(F, p_bc(F, t_dg[F]))
+    for P in range(H + 1):
+        v_E(P, H)
+    for F in range(H + 1, N):
+        v_E(H - 1, F)
+        v_E(H, F)
+    s_cnt(H - 1, N - 1)
+    s_cnt(H, N - 1)
+    total(H)
+    for X in range(H + 1, N):
+        for F in range(X, N):
+            v_E(X, F)
+        if X == H + 1:
+            v_idx(H - 1)
+        s_cnt(X, N - 1)
+        for P in range(X):
+            v_E(P, X)
+        if X == H + 1:
+            v_idx(H)
+        v_idx(X)
+        total(X)
 
     for j in range(FLY):
         need_sem("g", "zs%d" % j, ztot[j])
     for F in range(N):
+        if F == H - 1:
+            g.wait_ge(S.se, 16)
         if F == H:
-            g.wait_ge(S.sc, 16 * H)
+            g.wait_ge(S.sc, 16 * (H - 2))
         need("g", t_oc[F], t_idx[F])
         g.indirect_dma_start(out=T.y[:], out_offset=IndirectOffsetOnAxis(ap=T.sidx[:, F:F + 1], axis=0),
                              in_=T.outb[:, F * 64:(F + 1) * 64], in_offset=None,
-                             bounds_check=T.y.shape[0] - 1, oob_is_err=False).then_inc(S.sc, 16)
-    g.wait_ge(S.sc, 16 * N)
+                             bounds_check=T.y.shape[0] - 1, oob_is_err=False) \
+            .then_inc(S.se if F == 0 else S.sc if F < H - 1 else S.sd, 16)
+    g.wait_ge(S.sd, 16 * (N - H + 1))
     g.wait_ge(S.sent, nsent)
     finish()
     for s in range(N):

from concourse.bass import IndirectOffsetOnAxis, DstId, RemoteDMATransfer
from concourse.mybir import AluOpType, ActivationFunctionType

CW = 68
NB = 65
NSL = 16
HEAD = 3
FLY = 4
BIG = 32768.0

SCRATCH = {
    "idxs": ("sbuf", [128, 4], "int32"),
    "owni": ("sbuf", [128, 4], "int32"),
    "loci": ("sbuf", [128, 4], "int32"),
    "ownf": ("sbuf", [128, 4], "float32"),
    "locf": ("sbuf", [128, 4], "float32"),
    "numb": ("sbuf", [128, 4], "float32"),
    "raw": ("sbuf", [128, 4 * CW], "float32"),
    "io8": ("sbuf", [128, 8], "float32"),
    "io1": ("sbuf", [128, 128], "float32"),
    "onesf": ("sbuf", [128, 128], "float32"),
    "onesb": ("sbuf", [128, 128], "bfloat16"),
    "lb": ("sbuf", [128, 128], "bfloat16"),
    "ident": ("sbuf", [128, 128], "float32"),
    "mge": ("sbuf", [128, 128], "float32"),
    "oh8": ("sbuf", [128, 32], "bfloat16"),
    "place": ("sbuf", [128, 32], "float32"),
    "pmat": ("sbuf", [128, 16 * 128], "float32"),
    "sendb": ("sbuf", [128, 4 * CW], "float32"),
    "land": ("sbuf", [128, 8 * CW], "float32"),
    "diag": ("sbuf", [128, 1024], "float32"),
    "rowb": ("sbuf", [128, 1024], "float32"),
    "eq": ("sbuf", [128, 36 * 128], "float32"),
    "junk": ("sbuf", [128, 36 * 128], "float32"),
    "cnt": ("sbuf", [128, 8], "float32"),
    "vm": ("sbuf", [128, 8], "float32"),
    "sidx": ("sbuf", [128, 8], "int32"),
    "outb": ("sbuf", [128, 512], "float32"),
    "z": ("sbuf", [128, 2048], "float32"),
    "ppre": ("psum", [128, 512], "float32"),
    "pc0": ("psum", [128, 512], "float32"),
    "pc1": ("psum", [128, 512], "float32"),
    "pb0": ("psum", [128, 512], "float32"),
    "pb1": ("psum", [128, 512], "float32"),
    "pg0": ("psum", [128, 512], "float32"),
    "pg1": ("psum", [128, 512], "float32"),
    "pg2": ("psum", [128, 512], "float32"),
}
SEMAPHORES = ["sv", "sp", "ss", "sg", "lidx", "lgr", "zs0", "zs1", "zs2", "zs3", "gate", "sent", "fin0", "fin", "fout",
              "se", "sc", "sd"] + ["arr%d" % s for s in range(8)] + ["arn%d" % s for s in range(8)]


def _low(mask, n):
    out, k, b = 0, 0, 0
    while k < n:
        if (mask >> b) & 1:
            out |= 1 << b
            k += 1
        b += 1
    return out


def rank_program(g, core, T, topo):
    cores = [int(c) for c in T.cores]
    N = len(cores)
    S = T.sem
    NE = 8
    A = AluOpType
    ACT = ActivationFunctionType
    V, PE, SC = g.vector, g.tensor, g.scalar

    def split(r):
        me = cores[r]
        far = sorted([d for d in range(N) if d != r and not topo.may_write(me, cores[d])], key=lambda d: (d - r) % N)
        near = sorted([d for d in range(N) if d != r and topo.may_write(me, cores[d])], key=lambda d: (d - r) % N)
        return far, near

    def helper(r, d):
        me = cores[r]
        far, _ = split(r)
        hs = [h for h in range(topo.CORES_PER_CHIP * topo.CHIPS)
              if topo.chip(h) == topo.chip(me) and T.rank_of(h) is None and topo.may_write(h, cores[d])]
        return hs[far.index(d) % len(hs)]

    def chunks(x):
        est = {}
        for s in range(N):
            far, near = split(s)
            if s == x:
                est[s] = 0.0
            elif x in near:
                est[s] = 1.0 + near.index(x)
            else:
                est[s] = 100.0 + far.index(x)
        return sorted(range(N), key=lambda s: (est[s], s))

    def write(dst, out_ap, in_ap, rsem, lsem):
        rid, pid, _ = topo.addr(dst)
        g.remote_dma(out_ap=out_ap, in_ap=in_ap, remote_sem=rsem, local_sem=lsem, pid=pid, routing_id=rid,
                     dma_engine_mask=_low(topo.mask(core, dst), NE))

    def fan(dsts, buf, rsem, lsem):
        m = topo.mask(core, dsts[0])
        for h in dsts:
            m &= topo.mask(core, h)
        g.remote_dma_fused([RemoteDMATransfer(dst_ids=[DstId(rid=topo.addr(h)[0], pnc=topo.addr(h)[1]) for h in dsts],
                                              dma_engine_mask=m, remote_sem=rsem, srcs=[buf[:]],
                                              dsts=[buf[:] for h in dsts], alu_op=0)], local_sem=lsem)
        return bin(m).count("1")

    Q = {"v": g.vector, "p": g.tensor, "s": g.scalar, "g": g, "y": g.sync}
    SQ = {"v": S.sv, "p": S.sp, "s": S.ss, "g": S.sg}
    num = {"v": 0, "p": 0, "s": 0, "g": 0}
    seen = {}

    def done(q, ins):
        num[q] += 1
        ins.then_inc(SQ[q], 1)
        return (q, num[q])

    def need(q, *tickets):
        for (src, val) in tickets:
            if seen.get((q, src), 0) < val:
                Q[q].wait_ge(SQ[src], val)
                seen[(q, src)] = val

    def need_sem(q, name, val):
        if seen.get((q, name), 0) < val:
            Q[q].wait_ge(S[name], val)
            seen[(q, name)] = val

    def running_count(w, t_in):
        need("p", t_in)
        done("p", PE.matmul(T.ppre[:, 0:4 * w], T.lb[:], T.oh8[:, 0:4 * w], True, False))
        for k in (1, 2, 3):
            t = done("p", PE.matmul(T.ppre[:, k * w:4 * w], T.onesb[:], T.oh8[:, 0:(4 - k) * w], False, k == 3))
        need("v", t, t_in)
        t = done("v", V.tensor_tensor(T.place[:, 0:4 * w], T.oh8[:, 0:4 * w], T.ppre[:, 0:4 * w], A.mult))
        need("v", t)

    def pmats(di, col):
        tp = []
        for c in range(4):
            b = (di * 4 + c) * 128
            tp.append(done("v", V.tensor_scalar(T.pmat[:, b:b + 128], T.io1[:], T.place[:, col(c):col(c) + 1],
                                                None, A.is_equal)))
        return tp

    def collect(di, tp, ps, n, rhs, out_ap, before):
        need("p", *before)
        for c in range(4):
            b = (di * 4 + c) * 128
            need("p", tp[c])
            t = done("p", PE.matmul(ps[:, 0:n], T.pmat[:, b:b + 128], rhs(c), c == 0, c == 3))
        need("s", t)
        return done("s", SC.activation(out_ap, ps[:, 0:n], ACT.Copy))

    def finish():
        for q in ("v", "p", "s", "g"):
            need("g", (q, num[q]))

    rank = T.rank_of(core)
    if rank is None:
        jobs = [(r, d) for r in range(N) if topo.chip(cores[r]) == topo.chip(core)
                for d in split(r)[0] if helper(r, d) == core]
        for (r, d) in jobs:
            hs = [helper(r, x) for x in split(r)[0]]
            src = cores[r] if core == hs[0] else hs[0]
            nin0 = bin(topo.mask(cores[r], core)).count("1")
            nin = bin(topo.mask(src, core)).count("1")
            k = chunks(d).index(r)
            t_ob = done("v", V.memset(T.onesb[:], 1.0))
            need("g", t_ob)
            t_lb = done("g", g.affine_select(T.lb[:], T.onesb[:], [[1, 128]], A.is_ge, 0.0, 0, -1))
            t_io1 = done("g", g.iota(T.io1[:], [[1, 128]], 1, 0, allow_small_or_imprecise_dtypes=True))
            need("v", t_io1)
            need("p", t_lb)
            need_sem("v", "fin0", nin0)
            done("v", V.tensor_scalar(T.owni[:], T.idxs[:], 14, None, A.arith_shift_right))
            t = done("v", V.tensor_scalar(T.loci[:], T.idxs[:], 16383, None, A.bitwise_and))
            need("v", t)
            t = done("v", V.tensor_scalar(T.oh8[:, 0:4], T.owni[:], float(d), None, A.is_equal))
            t_lf = done("v", V.tensor_scalar(T.locf[:], T.loci[:], 1.0, None, A.add))
            running_count(1, t)
            tp = pmats(0, lambda c: c)
            t = collect(0, tp, T.pc1, 1, lambda c: T.locf[:, c:c + 1], T.numb[:, 0:1], [t_lf])
            need("g", t)
            write(cores[d], T.land[:, k * CW + 64:k * CW + 65], T.numb[:, 0:1], S["arn%d" % r], S.fout)
            nout = NE
            if core == hs[0] and len(hs) > 1:
                need_sem("g", "fin", nin)
                nout += fan(hs[1:], T.raw, S.fin, S.fout)
            need_sem("p", "fin", nin)
            t = collect(0, tp, T.pc0, 64, lambda c: T.raw[:, c * CW:c * CW + 64], T.sendb[:, 0:64], [])
            need("g", t)
            write(cores[d], T.land[:, k * CW:k * CW + 64], T.sendb[:, 0:64], S["arr%d" % r], S.fout)
            nout += NE
            g.wait_ge(S.fout, nout)
            finish()
        return

    rows = T.y.shape[0] // NSL
    far, near = split(rank)

    g.sync.dma_start(T.idxs[:], T.idx[:]).then_inc(S.lidx, 16)
    for c in range(4):
        SC.dma_start(T.raw[:, c * CW:c * CW + 64], T.gr[c * 128:(c + 1) * 128, :]).then_inc(S.lgr, 16)
    t_z = done("v", V.memset(T.z[:, 0:512], 0.0))
    t_ob = done("v", V.memset(T.onesb[:], 1.0))
    for c in range(4):
        t_pad = done("v", V.memset(T.raw[:, c * CW + 64:(c + 1) * CW], 0.0))
    t_of = done("v", V.memset(T.onesf[:], 1.0))
    need("s", t_z)
    for k in range(1, 4):
        t_ze = done("s", SC.activation(T.z[0:32, 512 * k:512 * (k + 1)], T.z[0:32, 0:512], ACT.Copy))
    t_io8 = done("g", g.iota(T.io8[:], [[1, 8]], 0, 0, allow_small_or_imprecise_dtypes=True))
    need("g", t_ob)
    t_lb = done("g", g.affine_select(T.lb[:], T.onesb[:], [[1, 128]], A.is_ge, 0.0, 0, -1))

    ztot = [0] * FLY
    need("y", t_z)
    for i in range(NSL):
        j = i % FLY
        if i >= HEAD:
            need("y", t_ze)
            need_sem("y", "gate", 1)
        if i >= FLY:
            need_sem("y", "zs%d" % j, ztot[j])
        g.sync.dma_start(T.y[i * rows:(i + 1) * rows, :], T.z[:, 0:512] if i < HEAD else T.z[0:32, 0:2048]) \
            .then_inc(S["zs%d" % j], 16)
        ztot[j] += 16

    hs = [helper(rank, d) for d in far]
    need_sem("g", "lidx", 16)
    nsent = fan(hs, T.idxs, S.fin0, S.sent)
    t_io1 = done("g", g.iota(T.io1[:], [[1, 128]], 1, 0, allow_small_or_imprecise_dtypes=True))

    need_sem("v", "lidx", 16)
    done("v", V.tensor_scalar(T.owni[:], T.idxs[:], 14, None, A.arith_shift_right))
    t = done("v", V.tensor_scalar(T.loci[:], T.idxs[:], 16383, None, A.bitwise_and))
    need("v", t, t_pad)
    t = done("v", V.tensor_copy(T.ownf[:], T.owni[:]))
    t_loc = done("v", V.tensor_scalar(T.raw[:, 64:4 * CW:CW], T.loci[:], 1.0, None, A.add))
    need("v", t, t_io8)
    for c in range(4):
        t_oh = done("v", V.tensor_scalar(T.oh8[:, c * 8:(c + 1) * 8], T.io8[:], T.ownf[:, c:c + 1], None, A.is_equal))

    need("g", t_loc)
    need_sem("g", "lgr", 64)
    nsent += fan(hs[0:1], T.raw, S.fin, S.sent)
    g.sem_inc(S.gate, 1)
    need("g", t_of)
    t_id = done("g", g.affine_select(T.ident[:], T.onesf[:], [[-1, 128]], A.is_equal, 0.0, 0, 1))
    t_mge = done("g", g.affine_select(T.mge[:], T.onesf[:], [[1, 128]], A.is_ge, 0.0, 0, -1))

    need("p", t_lb)
    running_count(8, t_oh)
    need("v", t_io1)

    mych = chunks(rank)
    pc = [T.pc0, T.pc1]
    t_cp = {}
    need_sem("p", "lgr", 64)
    need("p", t_loc)

    def rawc(c):
        return T.raw[:, c * CW:c * CW + NB]

    for di, d in enumerate(near + [rank]):
        before = [t_cp[di - 2]] if di >= 2 else []
        tp = pmats(di, lambda c: c * 8 + d)
        if d == rank:
            k = mych.index(rank)
            t_cp[di] = collect(di, tp, pc[di % 2], NB, rawc, T.land[:, k * CW:k * CW + NB], before)
            t_own = t_cp[di]
            continue
        t_cp[di] = collect(di, tp, pc[di % 2], NB, rawc, T.sendb[:, di * CW:di * CW + NB], before)
        need("g", t_cp[di])
        k = chunks(d).index(rank)
        write(cores[d], T.land[:, k * CW:k * CW + NB], T.sendb[:, di * CW:di * CW + NB], S["arr%d" % rank], S.sent)
        nsent += NE

    H = N - len(far)

    def arrive(q, P, what):
        if mych[P] == rank:
            need(q, t_own)
        elif P < H or what == "data":
            need_sem(q, "arr%d" % mych[P], NE)
        else:
            need_sem(q, "arn%d" % mych[P], NE)

    def val(P):
        return T.land[:, P * CW + 64:P * CW + 65]

    def blk(P, F):
        return (P * N - P * (P - 1) // 2 + F - P) * 128

    def eqb(P, F):
        return T.eq[:, blk(P, F):blk(P, F) + 128]

    pb = [T.pb0, T.pb1]
    bank = [T.pg0, T.pg1, T.pg2, T.ppre, T.pc0, T.pc1, T.pb0, T.pb1]
    t_E, t_bcc, t_vm, t_cnt, t_idx, t_oc, t_mm = {}, {}, {}, {}, {}, {}, {}

    def v_diag(P):
        arrive("v", P, "numbers")
        need("v", t_id)
        t = done("v", V.tensor_scalar(T.diag[:, P * 128:(P + 1) * 128], T.ident[:], val(P), None, A.mult))
        t_vm[P] = done("v", V.tensor_scalar(T.vm[:, P:P + 1], val(P), -(1.0 + BIG), None, A.add))
        return t

    def p_bc(P, t_d):
        need("p", t_d)
        if P >= 2:
            need("p", t_bcc[P - 2])
        return done("p", PE.matmul(pb[P % 2][:, 0:128], T.onesf[:], T.diag[:, P * 128:(P + 1) * 128], True, True))

    def s_bcc(P, t_b):
        need("s", t_b)
        t_bcc[P] = done("s", SC.activation(T.rowb[:, P * 128:(P + 1) * 128], pb[P % 2][:, 0:128], ACT.Copy))

    def v_E(P, F):
        if (P, F) in t_E:
            return
        arrive("v", P, "numbers")
        need("v", t_bcc[F])
        t_E[(P, F)] = done("v", V.tensor_scalar(eqb(P, F), T.rowb[:, F * 128:(F + 1) * 128], val(P), None, A.is_equal))
        if P == F:
            need("v", t_E[(P, F)], t_mge)
            t_E[(P, F)] = done("v", V.tensor_tensor(eqb(P, F), eqb(P, F), T.mge[:], A.mult))

    def s_cnt(P, F1):
        b, n = blk(P, P), (F1 - P + 1) * 128
        need("s", *[t_E[(P, F)] for F in range(P, F1 + 1)])
        t_cnt[P] = done("s", SC.activation(T.junk[:, b:b + n], T.eq[:, b:b + n], ACT.Copy,
                                           accum_out=T.cnt[:, P:P + 1]))

    def v_idx(P):
        need("v", t_cnt[P], t_vm[P])
        t_idx[P] = done("v", V.tensor_scalar(T.sidx[:, P:P + 1], T.cnt[:, P:P + 1], BIG, T.vm[:, P:P + 1],
                                             A.mult, A.add))

    def total(F):
        for P in range(F + 1):
            arrive("p", P, "data")
            need("p", t_E[(P, F)])
            if F >= N - 2:
                need("p", t_bcc[N - 2], t_bcc[N - 1])
            t = done("p", PE.matmul(bank[F][:, 0:64], eqb(P, F), T.land[:, P * CW:P * CW + 64], P == 0, P == F))
        need("s", t)
        t_oc[F] = done("s", SC.activation(T.outb[:, F * 64:(F + 1) * 64], bank[F][:, 0:64], ACT.Copy))

    need("p", *[t_cp[k] for k in t_cp])
    t_dg = {0: v_diag(0)}
    for F in range(H - 1):
        s_bcc(F, p_bc(F, t_dg[F]))
        if F + 1 < H - 1:
            t_dg[F + 1] = v_diag(F + 1)
        for P in range(F + 1):
            v_E(P, F)
    s_cnt(0, H - 2)
    v_idx(0)
    total(0)
    s_bcc(H - 1, p_bc(H - 1, v_diag(H - 1)))
    for P in range(H):
        v_E(P, H - 1)
    for F in range(1, H):
        if F < H - 1:
            s_cnt(F, H - 1)
            v_idx(F)
        total(F)
    for F in range(H, N):
        t_dg[F] = v_diag(F)
    for F in range(H, N):
        s_bcc(F, p_bc(F, t_dg[F]))
    for P in range(H + 1):
        v_E(P, H)
    for F in range(H + 1, N):
        v_E(H - 1, F)
        v_E(H, F)
    s_cnt(H - 1, N - 1)
    s_cnt(H, N - 1)
    total(H)
    for X in range(H + 1, N):
        for F in range(X, N):
            v_E(X, F)
        if X == H + 1:
            v_idx(H - 1)
        s_cnt(X, N - 1)
        for P in range(X):
            v_E(P, X)
        if X == H + 1:
            v_idx(H)
        v_idx(X)
        total(X)

    for j in range(FLY):
        need_sem("g", "zs%d" % j, ztot[j])
    for F in range(N):
        if F == H - 1:
            g.wait_ge(S.se, 16)
        if F == H:
            g.wait_ge(S.sc, 16 * (H - 2))
        need("g", t_oc[F], t_idx[F])
        g.indirect_dma_start(out=T.y[:], out_offset=IndirectOffsetOnAxis(ap=T.sidx[:, F:F + 1], axis=0),
                             in_=T.outb[:, F * 64:(F + 1) * 64], in_offset=None,
                             bounds_check=T.y.shape[0] - 1, oob_is_err=False) \
            .then_inc(S.se if F == 0 else S.sc if F < H - 1 else S.sd, 16)
    g.wait_ge(S.sd, 16 * (N - H + 1))
    g.wait_ge(S.sent, nsent)
    finish()
    for s in range(N):
        if s != rank:
            need_sem("g", "arr%d" % s, NE)
        if s in far:
            need_sem("g", "arn%d" % s, NE)
